import numpy as np
import ml_dtypes


def mxq(x, axis, fmt="e4m3"):
    dtype, down = {"e4m3": (ml_dtypes.float8_e4m3fn, 7), "e5m2": (ml_dtypes.float8_e5m2, 14)}[fmt]
    v = np.moveaxis(np.asarray(x, np.float32).astype(ml_dtypes.bfloat16).astype(np.float64), axis, -1)
    blocks = v.reshape(v.shape[:-1] + (-1, 32))
    amax = np.abs(blocks).max(-1, keepdims=True)
    byte = np.maximum(np.where(amax > 0, np.frexp(amax)[1] - 1 + 127, 0) - down, 1)
    scale = np.exp2(byte - 127.0)
    codes = (blocks / scale).astype(np.float32).astype(dtype).astype(np.float64)
    return np.moveaxis((codes * scale).reshape(v.shape), -1, axis)


WIDE = False


def mx_kscale(k):
    if not WIDE:
        return np.ones(k)
    levels = np.array([10, -10, 5, -5, 0])
    if k % 512:
        return np.exp2(np.random.permutation(np.resize(levels, k // 32))).repeat(32)
    a = np.empty((k // 512, 16))
    for p in range(k // 512):
        a[p, :8] = np.random.permutation(np.resize(levels, 8))
        for g in range(8):
            far = levels[np.abs(levels - a[p, g]) >= 10]
            a[p, g + 8] = far[np.random.randint(len(far))]
    return np.exp2(a.ravel()).repeat(32)


def f64(x):
    return np.asarray(x).astype(np.float64)


def striped8(idx):
    return np.asarray(idx).reshape(8, -1, 16).transpose(0, 2, 1).reshape(128, -1).astype(np.uint16)


def unstriped8(offs):
    return offs.reshape(8, 16, -1).transpose(0, 2, 1).reshape(8, -1).astype(np.int64)


def pick8(x, idx, run):
    r = np.arange(len(x))
    return x[r[:, None], idx[r % (8 * run) // run]]


E2M1 = np.array([0.0, 0.5, 1.0, 1.5, 2.0, 3.0, 4.0, 6.0, -0.0, -0.5, -1.0, -1.5, -2.0, -3.0, -4.0, -6.0])


def pack_weight(w, fmt):
    k, n = w.shape
    w = f64(np.asarray(w, np.float32).astype(ml_dtypes.bfloat16)).reshape(k // 32, 32, n)
    amax = np.abs(w).max(1)
    if fmt == "e4m3":
        byte = np.frexp(amax)[1] - 1 + 127 - 7
    else:
        mant, ex = np.frexp(amax / 6.0)
        byte = np.where(mant > 0.5, ex, ex - 1) + 127
    byte = np.clip(np.where(amax > 0, byte, 1), 1, 254)
    scaled = (w * np.exp2(127.0 - byte)[:, None, :]).reshape(k, n).astype(np.float32)
    by_word = np.ascontiguousarray(scaled.reshape(k // 512, 128, 4, n).transpose(0, 1, 3, 2))
    if fmt == "e4m3":
        words = by_word.astype(ml_dtypes.float8_e4m3fn).view(np.uint8)
    else:
        c = by_word.astype(ml_dtypes.float4_e2m1fn).view(np.uint8) & 0xF
        words = (c[..., 0::2] | (c[..., 1::2] << 4)).reshape(k // 512, 128, 2 * n)
    return np.ascontiguousarray(words), np.ascontiguousarray(byte.astype(np.uint8).reshape(k // 512, 16, n))


def unpack_weight(words, scales, fmt):
    g, _, n = scales.shape
    words = np.ascontiguousarray(words).reshape(g, 128, n, -1)
    if fmt == "e4m3":
        vals = words.view(ml_dtypes.float8_e4m3fn).astype(np.float64)
    else:
        nib = np.empty((g, 128, n, 4), np.uint8)
        nib[..., 0::2] = words & 0xF
        nib[..., 1::2] = words >> 4
        vals = E2M1[nib]
    vals = vals * np.repeat(np.exp2(scales.astype(np.float64) - 127.0), 8, axis=1)[..., None]
    return vals.transpose(0, 1, 3, 2).reshape(g * 512, n)


D, T, I, Q = 512, 1024, 512, 128


def setup_inputs():
    n = np.random.standard_normal
    idx = np.stack([np.random.permutation(T)[:I] for _ in range(8)])
    idx2 = np.stack([np.random.permutation(T)[:I] for _ in range(8)])
    idx3 = np.stack([np.random.permutation(T)[:I] for _ in range(8)])
    idx4 = np.stack([np.random.permutation(T)[:I] for _ in range(8)])
    fd = mx_kscale(D)
    keysp = pack_weight(n((D, T)) / fd[:, None], "e4m3")
    return {
        "query": (n((D, Q)) * 0.9 / np.sqrt(D) * fd[:, None]).astype(np.float32),
        "query2": (n((D, Q)) * 0.9 / np.sqrt(D) * fd[:, None]).astype(np.float32),
        "keys_words": keysp[0],
        "keys_scales": keysp[1],
        "lam": (np.random.uniform(0.5, 1.3, (Q, 1))).astype(np.float32),
        "old": (np.random.uniform(0.3, 1.7, (Q, T))).astype(np.float32),
        "base": (0.5 * n((Q, T))).astype(np.float32),
        "offs": striped8(idx),
        "offs2": striped8(idx2),
        "offs3": striped8(idx3),
        "offs4": striped8(idx4),
    }


def reference(query, query2, keys_words, keys_scales, lam, old, base, offs, offs2, offs3, offs4):
    idx = unstriped8(offs)
    idx2 = unstriped8(offs2)
    idx3 = unstriped8(offs3)
    idx4 = unstriped8(offs4)
    keysu = unpack_weight(keys_words, keys_scales, "e4m3")
    queryq = mxq(f64(query), 0, "e4m3")
    a = queryq.T @ keysu
    query2q = mxq(f64(query2), 0, "e4m3")
    b = query2q.T @ keysu
    w = (np.maximum(pick8(a, idx, 16), pick8(b, idx2, 16)) - np.maximum(pick8(a, idx2, 16), pick8(b, idx, 16))) * f64(lam)
    ws = w * pick8(f64(old), idx3, 16)
    f1 = np.zeros((Q, T))
    f1[np.arange(Q)[:, None], idx4[np.arange(Q) % 128 // 16]] = ws
    y = f64(base) + f1
    return y

@@ -1,0 +1,132 @@
+from contextlib import ExitStack
+
+import concourse.mybir as mybir
+
+D, T, I, Q = 512, 1024, 512, 128
+FLOPS = 2 * 2 * D * T * Q
+
+F32 = mybir.dt.float32
+BF16 = mybir.dt.bfloat16
+I32 = mybir.dt.int32
+U32 = mybir.dt.uint32
+U16 = mybir.dt.uint16
+U8 = mybir.dt.uint8
+FP8X4 = mybir.dt.float8_e4m3fn_x4
+ALU = mybir.AluOpType
+COPY = mybir.ActivationFunctionType.Copy
+
+P = 128
+PACK = 4
+BANK = 512
+HALF = I // 2
+LIST_COLS = I // 16
+STORE = 256
+
+
+def tile_attend_exchanged_lean_timesold_heads_kernel(
+    tc, query, query2, keys_words, keys_scales, lam, old, base, offs, offs2, offs3, offs4, out
+):
+    nc = tc.nc
+    with ExitStack() as ctx:
+        sb = ctx.enter_context(tc.tile_pool(name="sb", bufs=1))
+        ps = ctx.enter_context(tc.psum_pool(name="ps", bufs=1))
+
+        key_scale = sb.tile([P, T], U8, name="key_scale", align_bytes=64)
+        nc.vector.memset(key_scale[:].bitcast(I32), 0)
+        placed = sb.tile([P, T], F32, name="placed")
+        nc.gpsimd.memset(placed[:], 0.0)
+
+        raw = [sb.tile([P, PACK, Q], F32, name="raw%d" % s) for s in range(2)]
+        for s, src in enumerate((query, query2)):
+            nc.sync.dma_start(out=raw[s][:], in_=src.rearrange("(p j) q -> p j q", j=PACK))
+        for quad in range(4):
+            nc.scalar.dma_start(
+                out=key_scale[32 * quad : 32 * quad + 4, :].bitcast(I32),
+                in_=keys_scales[0, 4 * quad : 4 * quad + 4, :].bitcast(I32),
+            )
+        words = keys_words[0].rearrange("p n t -> p (n t)").bitcast(I32)
+        key_code = [sb.tile([P, BANK], U32, name="key_code%d" % c, align_bytes=64) for c in range(2)]
+        for c in range(2):
+            nc.sync.dma_start(out=key_code[c][:].bitcast(I32), in_=words[:, c * BANK : (c + 1) * BANK])
+        list1 = sb.tile([P, LIST_COLS], U16, name="list1")
+        list2 = sb.tile([P, LIST_COLS], U16, name="list2")
+        list3 = sb.tile([P, LIST_COLS], U16, name="list3")
+        list4 = sb.tile([P, LIST_COLS], U16, name="list4")
+        old_sb = sb.tile([P, T], F32, name="old_sb")
+        base_sb = sb.tile([P, T], F32, name="base_sb")
+        lam_sb = sb.tile([P, 1], F32, name="lam_sb")
+        nc.sync.dma_start(list1[:], offs)
+        nc.sync.dma_start(list2[:], offs2)
+        nc.sync.dma_start(out=old_sb[:], in_=old)
+        nc.sync.dma_start(list3[:], offs3)
+        nc.sync.dma_start(list4[:], offs4)
+        nc.sync.dma_start(out=lam_sb[:], in_=lam)
+        nc.sync.dma_start(out=base_sb[:], in_=base)
+
+        q_code, q_scale = [], []
+        grouped = [sb.tile([P, Q, PACK], BF16, name="grouped%d" % s, align_bytes=64) for s in range(2)]
+        for s in range(2):
+            nc.vector.tensor_copy(out=grouped[s][:], in_=raw[s][:].rearrange("p j q -> p q j"))
+        for s in range(2):
+            code = sb.tile([P, Q], U32, name="q_code%d" % s, align_bytes=64)
+            scale = sb.tile([P, Q], U8, name="q_scale%d" % s, align_bytes=64)
+            nc.vector.quantize_mx(
+                out=code[:].bitcast(FP8X4), scales=scale[:], in_=grouped[s][:].rearrange("p q j -> p (q j)")
+            )
+            q_code.append(code)
+            q_scale.append(scale)
+
+        score = [sb.tile([P, T], F32, name="score%d" % s) for s in range(2)]
+        for s in range(2):
+            for c in range(2):
+                cols = slice(c * BANK, (c + 1) * BANK)
+                acc = ps.tile([P, BANK], F32, name="acc%d%d" % (s, c))
+                nc.tensor.matmul_mx(
+                    out=acc[:],
+                    lhsT=q_code[s][:].bitcast(FP8X4),
+                    lhsT_scale=q_scale[s][:],
+                    rhs=key_code[c][:].bitcast(FP8X4),
+                    rhs_scale=key_scale[:, cols],
+                    start=True,
+                    stop=True,
+                )
+                if s == 0 and c == 0:
+                    nc.vector.tensor_copy(out=score[s][:, cols], in_=acc[:])
+                else:
+                    nc.scalar.activation(score[s][:, cols], acc[:], COPY)
+        a, b = score
+
+        def gather(on_vector, dst, window, lst, h):
+            src = window[:].indirect(lst[:, h * (HALF // 16) : (h + 1) * (HALF // 16)])
+            if on_vector:
+                nc.vector.tensor_copy(dst, src)
+            else:
+                nc.scalar.activation(dst, src, COPY)
+
+        for h in range(2):
+            from_a = sb.tile([P, 2, HALF], F32, name="from_a%d" % h)
+            from_b = sb.tile([P, 2, HALF], F32, name="from_b%d" % h)
+            from_old = sb.tile([P, HALF], F32, name="from_old%d" % h)
+            first = h == 0
+            gather(first, from_a[:, 0, :], a, list1, h)
+            gather(False, from_b[:, 0, :], b, list2, h)
+            gather(first, from_a[:, 1, :], a, list2, h)
+            gather(first, from_b[:, 1, :], b, list1, h)
+            gather(False, from_old[:], old_sb, list3, h)
+            larger = sb.tile([P, 2, HALF], F32, name="larger%d" % h)
+            nc.vector.tensor_tensor(larger[:], from_a[:], from_b[:], ALU.max)
+            diff = sb.tile([P, HALF], F32, name="diff%d" % h)
+            nc.vector.tensor_tensor(diff[:], larger[:, 0, :], larger[:, 1, :], ALU.subtract)
+            nc.vector.tensor_tensor(
+                placed[:].indirect(list4[:, h * (HALF // 16) : (h + 1) * (HALF // 16)]),
+                diff[:],
+                from_old[:],
+                ALU.mult,
+            )
+
+        for c in range(T // STORE):
+            cols = slice(c * STORE, (c + 1) * STORE)
+            res = sb.tile([P, STORE], F32, name="res%d" % c)
+            nc.vector.scalar_tensor_tensor(res[:], placed[:, cols], lam_sb[:], base_sb[:, cols], ALU.mult, ALU.add)
+            queue = nc.sync if c % 2 == 0 else nc.scalar
+            queue.dma_start(out=out[:, cols], in_=res[:])

@@ -32,22 +32,21 @@ def tile_attend_exchanged_lean_timesold_heads_kernel(
         ps = ctx.enter_context(tc.psum_pool(name="ps", bufs=1))
 
         key_scale = sb.tile([P, T], U8, name="key_scale", align_bytes=64)
-        nc.vector.memset(key_scale[:].bitcast(I32), 0)
         placed = sb.tile([P, T], F32, name="placed")
         nc.gpsimd.memset(placed[:], 0.0)
 
         raw = [sb.tile([P, PACK, Q], F32, name="raw%d" % s) for s in range(2)]
-        for s, src in enumerate((query, query2)):
-            nc.sync.dma_start(out=raw[s][:], in_=src.rearrange("(p j) q -> p j q", j=PACK))
+        nc.sync.dma_start(out=raw[0][:], in_=query.rearrange("(p j) q -> p j q", j=PACK))
         for quad in range(4):
-            nc.scalar.dma_start(
+            nc.sync.dma_start(
                 out=key_scale[32 * quad : 32 * quad + 4, :].bitcast(I32),
                 in_=keys_scales[0, 4 * quad : 4 * quad + 4, :].bitcast(I32),
             )
         words = keys_words[0].rearrange("p n t -> p (n t)").bitcast(I32)
-        key_code = [sb.tile([P, BANK], U32, name="key_code%d" % c, align_bytes=64) for c in range(2)]
-        for c in range(2):
-            nc.sync.dma_start(out=key_code[c][:].bitcast(I32), in_=words[:, c * BANK : (c + 1) * BANK])
+        key_code = [sb.tile([P, BANK], U32, name="key_code%d" % c, tag="keys%d" % c, align_bytes=64) for c in range(2)]
+        nc.sync.dma_start(out=key_code[0][:].bitcast(I32), in_=words[:, :BANK])
+        nc.sync.dma_start(out=raw[1][:], in_=query2.rearrange("(p j) q -> p j q", j=PACK))
+        nc.sync.dma_start(out=key_code[1][:].bitcast(I32), in_=words[:, BANK:])
         list1 = sb.tile([P, LIST_COLS], U16, name="list1")
         list2 = sb.tile([P, LIST_COLS], U16, name="list2")
         list3 = sb.tile([P, LIST_COLS], U16, name="list3")
@@ -67,7 +66,6 @@ def tile_attend_exchanged_lean_timesold_heads_kernel(
         grouped = [sb.tile([P, Q, PACK], BF16, name="grouped%d" % s, align_bytes=64) for s in range(2)]
         for s in range(2):
             nc.vector.tensor_copy(out=grouped[s][:], in_=raw[s][:].rearrange("p j q -> p q j"))
-        for s in range(2):
             code = sb.tile([P, Q], U32, name="q_code%d" % s, align_bytes=64)
             scale = sb.tile([P, Q], U8, name="q_scale%d" % s, align_bytes=64)
             nc.vector.quantize_mx(
@@ -77,20 +75,21 @@ def tile_attend_exchanged_lean_timesold_heads_kernel(
             q_scale.append(scale)
 
         score = [sb.tile([P, T], F32, name="score%d" % s) for s in range(2)]
+        pieces = [[(0, 512), (512, 256), (768, 256)], [(0, 256), (256, 256), (512, 256), (768, 256)]]
         for s in range(2):
-            for c in range(2):
-                cols = slice(c * BANK, (c + 1) * BANK)
-                acc = ps.tile([P, BANK], F32, name="acc%d%d" % (s, c))
+            for start, width in pieces[s]:
+                cols = slice(start, start + width)
+                acc = ps.tile([P, width], F32, name="acc%d_%d" % (s, start))
                 nc.tensor.matmul_mx(
                     out=acc[:],
                     lhsT=q_code[s][:].bitcast(FP8X4),
                     lhsT_scale=q_scale[s][:],
-                    rhs=key_code[c][:].bitcast(FP8X4),
+                    rhs=key_code[start // BANK][:, start % BANK : start % BANK + width].bitcast(FP8X4),
                     rhs_scale=key_scale[:, cols],
                     start=True,
                     stop=True,
                 )
-                if s == 0 and c == 0:
+                if s == 0 and start + width == T:
                     nc.vector.tensor_copy(out=score[s][:, cols], in_=acc[:])
                 else:
                     nc.scalar.activation(score[s][:, cols], acc[:], COPY)
@@ -103,26 +102,34 @@ def tile_attend_exchanged_lean_timesold_heads_kernel(
             else:
                 nc.scalar.activation(dst, src, COPY)
 
+        late = sb.tile([P, 3, HALF], F32, name="late", tag="keys1", align_bytes=64)
+        early_a = sb.tile([P, 2, HALF], F32, name="early_a")
+        from_a = [[early_a[:, 0, :], early_a[:, 1, :]], [late[:, 0, :], late[:, 1, :]]]
+        from_old = [late[:, 2, :], late[:, 2, :]]
+        from_b = [[sb.tile([P, HALF], F32, name="from_b%d%d" % (h, j))[:] for j in range(2)] for h in range(2)]
+        gather(True, from_a[0][0], a, list1, 0)
+        gather(True, from_a[0][1], a, list2, 0)
+        gather(True, from_b[0][1], b, list1, 0)
+        gather(False, from_b[0][0], b, list2, 0)
+        gather(False, from_a[1][0], a, list1, 1)
+        gather(False, from_old[0], old_sb, list3, 0)
+        gather(False, from_b[1][0], b, list2, 1)
+        gather(False, from_a[1][1], a, list2, 1)
+        gather(False, from_b[1][1], b, list1, 1)
+        larger = [sb.tile([P, HALF], F32, name="larger%d" % j) for j in range(2)]
         for h in range(2):
-            from_a = sb.tile([P, 2, HALF], F32, name="from_a%d" % h)
-            from_b = sb.tile([P, 2, HALF], F32, name="from_b%d" % h)
-            from_old = sb.tile([P, HALF], F32, name="from_old%d" % h)
-            first = h == 0
-            gather(first, from_a[:, 0, :], a, list1, h)
-            gather(False, from_b[:, 0, :], b, list2, h)
-            gather(first, from_a[:, 1, :], a, list2, h)
-            gather(first, from_b[:, 1, :], b, list1, h)
-            gather(False, from_old[:], old_sb, list3, h)
-            larger = sb.tile([P, 2, HALF], F32, name="larger%d" % h)
-            nc.vector.tensor_tensor(larger[:], from_a[:], from_b[:], ALU.max)
+            for j in range(2):
+                nc.vector.tensor_tensor(larger[j][:], from_a[h][j], from_b[h][j], ALU.max)
             diff = sb.tile([P, HALF], F32, name="diff%d" % h)
-            nc.vector.tensor_tensor(diff[:], larger[:, 0, :], larger[:, 1, :], ALU.subtract)
+            nc.vector.tensor_tensor(diff[:], larger[0][:], larger[1][:], ALU.subtract)
             nc.vector.tensor_tensor(
                 placed[:].indirect(list4[:, h * (HALF // 16) : (h + 1) * (HALF // 16)]),
                 diff[:],
-                from_old[:],
+                from_old[h],
                 ALU.mult,
             )
+            if h == 0:
+                gather(False, from_old[1], old_sb, list3, 1)
 
         for c in range(T // STORE):
             cols = slice(c * STORE, (c + 1) * STORE)

@@ -19,6 +19,7 @@ P = 128
 PACK = 4
 BANK = 512
 HALF = I // 2
+QUARTER = I // 4
 LIST_COLS = I // 16
 STORE = 256
 
@@ -102,34 +103,52 @@ def tile_attend_exchanged_lean_timesold_heads_kernel(
             else:
                 nc.scalar.activation(dst, src, COPY)
 
-        late = sb.tile([P, 3, HALF], F32, name="late", tag="keys1", align_bytes=64)
+        late = sb.tile([P, 2 * HALF + 3 * QUARTER], F32, name="late", tag="keys1", align_bytes=64)
         early_a = sb.tile([P, 2, HALF], F32, name="early_a")
-        from_a = [[early_a[:, 0, :], early_a[:, 1, :]], [late[:, 0, :], late[:, 1, :]]]
-        from_old = [late[:, 2, :], late[:, 2, :]]
+        from_a = [[early_a[:, 0, :], early_a[:, 1, :]], [late[:, :HALF], late[:, HALF : 2 * HALF]]]
+        from_old = [late[:, 2 * HALF + QUARTER :], late[:, 2 * HALF : 3 * HALF]]
         from_b = [[sb.tile([P, HALF], F32, name="from_b%d%d" % (h, j))[:] for j in range(2)] for h in range(2)]
         gather(True, from_a[0][0], a, list1, 0)
         gather(True, from_a[0][1], a, list2, 0)
         gather(True, from_b[0][1], b, list1, 0)
         gather(False, from_b[0][0], b, list2, 0)
-        gather(False, from_a[1][0], a, list1, 1)
         gather(False, from_old[0], old_sb, list3, 0)
+        gather(False, from_a[1][0], a, list1, 1)
         gather(False, from_b[1][0], b, list2, 1)
         gather(False, from_a[1][1], a, list2, 1)
         gather(False, from_b[1][1], b, list1, 1)
         larger = [sb.tile([P, HALF], F32, name="larger%d" % j) for j in range(2)]
-        for h in range(2):
-            for j in range(2):
-                nc.vector.tensor_tensor(larger[j][:], from_a[h][j], from_b[h][j], ALU.max)
-            diff = sb.tile([P, HALF], F32, name="diff%d" % h)
-            nc.vector.tensor_tensor(diff[:], larger[0][:], larger[1][:], ALU.subtract)
+        diff = [sb.tile([P, HALF], F32, name="diff%d" % h) for h in range(2)]
+        whole = slice(0, HALF)
+        quarters = [slice(0, QUARTER), slice(QUARTER, HALF)]
+
+        def take_max(h, j, cols):
+            nc.vector.tensor_tensor(larger[j][:, cols], from_a[h][j][:, cols], from_b[h][j][:, cols], ALU.max)
+
+        def subtract(h, cols):
+            nc.vector.tensor_tensor(diff[h][:, cols], larger[0][:, cols], larger[1][:, cols], ALU.subtract)
+
+        def scatter(h, cols):
+            first = (h * HALF + cols.start) // 16
+            last = (h * HALF + cols.stop) // 16
             nc.vector.tensor_tensor(
-                placed[:].indirect(list4[:, h * (HALF // 16) : (h + 1) * (HALF // 16)]),
-                diff[:],
-                from_old[h],
-                ALU.mult,
+                placed[:].indirect(list4[:, first:last]), diff[h][:, cols], from_old[h][:, cols], ALU.mult
             )
-            if h == 0:
-                gather(False, from_old[1], old_sb, list3, 1)
+
+        take_max(0, 1, whole)
+        for cols in quarters:
+            take_max(0, 0, cols)
+        for cols in quarters:
+            subtract(0, cols)
+        scatter(0, quarters[0])
+        take_max(1, 0, whole)
+        scatter(0, quarters[1])
+        gather(False, from_old[1], old_sb, list3, 1)
+        for cols in quarters:
+            take_max(1, 1, cols)
+        for cols in quarters:
+            subtract(1, cols)
+        scatter(1, whole)
 
         for c in range(T // STORE):
             cols = slice(c * STORE, (c + 1) * STORE)

@@ -21,7 +21,6 @@ BANK = 512
 HALF = I // 2
 QUARTER = I // 4
 LIST_COLS = I // 16
-STORE = 256
 
 
 def tile_attend_exchanged_lean_timesold_heads_kernel(
@@ -38,10 +37,10 @@ def tile_attend_exchanged_lean_timesold_heads_kernel(
 
         raw = [sb.tile([P, PACK, Q], F32, name="raw%d" % s) for s in range(2)]
         nc.sync.dma_start(out=raw[0][:], in_=query.rearrange("(p j) q -> p j q", j=PACK))
-        for quad in range(4):
+        for r in range(4):
             nc.sync.dma_start(
-                out=key_scale[32 * quad : 32 * quad + 4, :].bitcast(I32),
-                in_=keys_scales[0, 4 * quad : 4 * quad + 4, :].bitcast(I32),
+                out=key_scale[r:P:32, :].bitcast(I32),
+                in_=keys_scales[0, r:16:4, :].bitcast(I32),
             )
         words = keys_words[0].rearrange("p n t -> p (n t)").bitcast(I32)
         key_code = [sb.tile([P, BANK], U32, name="key_code%d" % c, tag="keys%d" % c, align_bytes=64) for c in range(2)]
@@ -150,9 +149,10 @@ def tile_attend_exchanged_lean_timesold_heads_kernel(
             subtract(1, cols)
         scatter(1, whole)
 
-        for c in range(T // STORE):
-            cols = slice(c * STORE, (c + 1) * STORE)
-            res = sb.tile([P, STORE], F32, name="res%d" % c)
+        edges = [0, 128, 384, 640, 896, T]
+        for c in range(len(edges) - 1):
+            cols = slice(edges[c], edges[c + 1])
+            res = sb.tile([P, edges[c + 1] - edges[c]], F32, name="res%d" % c)
             nc.vector.scalar_tensor_tensor(res[:], placed[:, cols], lam_sb[:], base_sb[:, cols], ALU.mult, ALU.add)
             queue = nc.sync if c % 2 == 0 else nc.scalar
             queue.dma_start(out=out[:, cols], in_=res[:])

@@ -33,7 +33,7 @@ def tile_attend_exchanged_lean_timesold_heads_kernel(
 
         key_scale = sb.tile([P, T], U8, name="key_scale", align_bytes=64)
         placed = sb.tile([P, T], F32, name="placed")
-        nc.gpsimd.memset(placed[:], 0.0)
+        nc.vector.memset(placed[:], 0.0)
 
         raw = [sb.tile([P, PACK, Q], F32, name="raw%d" % s) for s in range(2)]
         nc.sync.dma_start(out=raw[0][:], in_=query.rearrange("(p j) q -> p j q", j=PACK))
@@ -65,7 +65,10 @@ def tile_attend_exchanged_lean_timesold_heads_kernel(
         q_code, q_scale = [], []
         grouped = [sb.tile([P, Q, PACK], BF16, name="grouped%d" % s, align_bytes=64) for s in range(2)]
         for s in range(2):
-            nc.vector.tensor_copy(out=grouped[s][:], in_=raw[s][:].rearrange("p j q -> p q j"))
+            nc.vector.tensor_copy(
+                out=grouped[s][:].rearrange("p (c i) j -> p c j i", i=4),
+                in_=raw[s][:].rearrange("p j (c i) -> p c j i", i=4),
+            )
             code = sb.tile([P, Q], U32, name="q_code%d" % s, align_bytes=64)
             scale = sb.tile([P, Q], U8, name="q_scale%d" % s, align_bytes=64)
             nc.vector.quantize_mx(

from contextlib import ExitStack

import concourse.mybir as mybir

D, T, I, Q = 512, 1024, 512, 128
FLOPS = 2 * 2 * D * T * Q

F32 = mybir.dt.float32
BF16 = mybir.dt.bfloat16
I32 = mybir.dt.int32
U32 = mybir.dt.uint32
U16 = mybir.dt.uint16
U8 = mybir.dt.uint8
FP8X4 = mybir.dt.float8_e4m3fn_x4
ALU = mybir.AluOpType
COPY = mybir.ActivationFunctionType.Copy

P = 128
PACK = 4
BANK = 512
HALF = I // 2
QUARTER = I // 4
LIST_COLS = I // 16


def tile_attend_exchanged_lean_timesold_heads_kernel(
    tc, query, query2, keys_words, keys_scales, lam, old, base, offs, offs2, offs3, offs4, out
):
    nc = tc.nc
    with ExitStack() as ctx:
        sb = ctx.enter_context(tc.tile_pool(name="sb", bufs=1))
        ps = ctx.enter_context(tc.psum_pool(name="ps", bufs=1))

        key_scale = sb.tile([P, T], U8, name="key_scale", align_bytes=64)
        placed = sb.tile([P, T], F32, name="placed")
        nc.vector.memset(placed[:], 0.0)

        raw = [sb.tile([P, PACK, Q], F32, name="raw%d" % s) for s in range(2)]
        nc.sync.dma_start(out=raw[0][:], in_=query.rearrange("(p j) q -> p j q", j=PACK))
        for r in range(4):
            nc.sync.dma_start(
                out=key_scale[r:P:32, :].bitcast(I32),
                in_=keys_scales[0, r:16:4, :].bitcast(I32),
            )
        words = keys_words[0].rearrange("p n t -> p (n t)").bitcast(I32)
        key_code = [sb.tile([P, BANK], U32, name="key_code%d" % c, tag="keys%d" % c, align_bytes=64) for c in range(2)]
        nc.sync.dma_start(out=key_code[0][:].bitcast(I32), in_=words[:, :BANK])
        nc.sync.dma_start(out=raw[1][:], in_=query2.rearrange("(p j) q -> p j q", j=PACK))
        nc.sync.dma_start(out=key_code[1][:].bitcast(I32), in_=words[:, BANK:])
        list1 = sb.tile([P, LIST_COLS], U16, name="list1")
        list2 = sb.tile([P, LIST_COLS], U16, name="list2")
        list3 = sb.tile([P, LIST_COLS], U16, name="list3")
        list4 = sb.tile([P, LIST_COLS], U16, name="list4")
        old_sb = sb.tile([P, T], F32, name="old_sb")
        base_sb = sb.tile([P, T], F32, name="base_sb")
        lam_sb = sb.tile([P, 1], F32, name="lam_sb")
        nc.sync.dma_start(list1[:], offs)
        nc.sync.dma_start(list2[:], offs2)
        nc.sync.dma_start(out=old_sb[:], in_=old)
        nc.sync.dma_start(list3[:], offs3)
        nc.sync.dma_start(list4[:], offs4)
        nc.sync.dma_start(out=lam_sb[:], in_=lam)
        nc.sync.dma_start(out=base_sb[:], in_=base)

        q_code, q_scale = [], []
        grouped = [sb.tile([P, Q, PACK], BF16, name="grouped%d" % s, align_bytes=64) for s in range(2)]
        for s in range(2):
            nc.vector.tensor_copy(
                out=grouped[s][:].rearrange("p (c i) j -> p c j i", i=4),
                in_=raw[s][:].rearrange("p j (c i) -> p c j i", i=4),
            )
            code = sb.tile([P, Q], U32, name="q_code%d" % s, align_bytes=64)
            scale = sb.tile([P, Q], U8, name="q_scale%d" % s, align_bytes=64)
            nc.vector.quantize_mx(
                out=code[:].bitcast(FP8X4), scales=scale[:], in_=grouped[s][:].rearrange("p q j -> p (q j)")
            )
            q_code.append(code)
            q_scale.append(scale)

        score = [sb.tile([P, T], F32, name="score%d" % s) for s in range(2)]
        pieces = [[(0, 512), (512, 256), (768, 256)], [(0, 256), (256, 256), (512, 256), (768, 256)]]
        for s in range(2):
            for start, width in pieces[s]:
                cols = slice(start, start + width)
                acc = ps.tile([P, width], F32, name="acc%d_%d" % (s, start))
                nc.tensor.matmul_mx(
                    out=acc[:],
                    lhsT=q_code[s][:].bitcast(FP8X4),
                    lhsT_scale=q_scale[s][:],
                    rhs=key_code[start // BANK][:, start % BANK : start % BANK + width].bitcast(FP8X4),
                    rhs_scale=key_scale[:, cols],
                    start=True,
                    stop=True,
                )
                if s == 0 and start + width == T:
                    nc.vector.tensor_copy(out=score[s][:, cols], in_=acc[:])
                else:
                    nc.scalar.activation(score[s][:, cols], acc[:], COPY)
        a, b = score

        def gather(on_vector, dst, window, lst, h):
            src = window[:].indirect(lst[:, h * (HALF // 16) : (h + 1) * (HALF // 16)])
            if on_vector:
                nc.vector.tensor_copy(dst, src)
            else:
                nc.scalar.activation(dst, src, COPY)

        late = sb.tile([P, 2 * HALF + 3 * QUARTER], F32, name="late", tag="keys1", align_bytes=64)
        early_a = sb.tile([P, 2, HALF], F32, name="early_a")
        from_a = [[early_a[:, 0, :], early_a[:, 1, :]], [late[:, :HALF], late[:, HALF : 2 * HALF]]]
        from_old = [late[:, 2 * HALF + QUARTER :], late[:, 2 * HALF : 3 * HALF]]
        from_b = [[sb.tile([P, HALF], F32, name="from_b%d%d" % (h, j))[:] for j in range(2)] for h in range(2)]
        gather(True, from_a[0][0], a, list1, 0)
        gather(True, from_a[0][1], a, list2, 0)
        gather(True, from_b[0][1], b, list1, 0)
        gather(False, from_b[0][0], b, list2, 0)
        gather(False, from_old[0], old_sb, list3, 0)
        gather(False, from_a[1][0], a, list1, 1)
        gather(False, from_b[1][0], b, list2, 1)
        gather(False, from_a[1][1], a, list2, 1)
        gather(False, from_b[1][1], b, list1, 1)
        larger = [sb.tile([P, HALF], F32, name="larger%d" % j) for j in range(2)]
        diff = [sb.tile([P, HALF], F32, name="diff%d" % h) for h in range(2)]
        whole = slice(0, HALF)
        quarters = [slice(0, QUARTER), slice(QUARTER, HALF)]

        def take_max(h, j, cols):
            nc.vector.tensor_tensor(larger[j][:, cols], from_a[h][j][:, cols], from_b[h][j][:, cols], ALU.max)

        def subtract(h, cols):
            nc.vector.tensor_tensor(diff[h][:, cols], larger[0][:, cols], larger[1][:, cols], ALU.subtract)

        def scatter(h, cols):
            first = (h * HALF + cols.start) // 16
            last = (h * HALF + cols.stop) // 16
            nc.vector.tensor_tensor(
                placed[:].indirect(list4[:, first:last]), diff[h][:, cols], from_old[h][:, cols], ALU.mult
            )

        take_max(0, 1, whole)
        for cols in quarters:
            take_max(0, 0, cols)
        for cols in quarters:
            subtract(0, cols)
        scatter(0, quarters[0])
        take_max(1, 0, whole)
        scatter(0, quarters[1])
        gather(False, from_old[1], old_sb, list3, 1)
        for cols in quarters:
            take_max(1, 1, cols)
        for cols in quarters:
            subtract(1, cols)
        scatter(1, whole)

        edges = [0, 128, 384, 640, 896, T]
        for c in range(len(edges) - 1):
            cols = slice(edges[c], edges[c + 1])
            res = sb.tile([P, edges[c + 1] - edges[c]], F32, name="res%d" % c)
            nc.vector.scalar_tensor_tensor(res[:], placed[:, cols], lam_sb[:], base_sb[:, cols], ALU.mult, ALU.add)
            queue = nc.sync if c % 2 == 0 else nc.scalar
            queue.dma_start(out=out[:, cols], in_=res[:])
